import numpy as np
import ml_dtypes


def mxq(x, axis, fmt="e4m3"):
    dtype, down = {"e4m3": (ml_dtypes.float8_e4m3fn, 7), "e5m2": (ml_dtypes.float8_e5m2, 14)}[fmt]
    v = np.moveaxis(np.asarray(x, np.float32).astype(ml_dtypes.bfloat16).astype(np.float64), axis, -1)
    blocks = v.reshape(v.shape[:-1] + (-1, 32))
    amax = np.abs(blocks).max(-1, keepdims=True)
    byte = np.maximum(np.where(amax > 0, np.frexp(amax)[1] - 1 + 127, 0) - down, 1)
    scale = np.exp2(byte - 127.0)
    codes = (blocks / scale).astype(np.float32).astype(dtype).astype(np.float64)
    return np.moveaxis((codes * scale).reshape(v.shape), -1, axis)


WIDE = False


def mx_kscale(k):
    if not WIDE:
        return np.ones(k)
    levels = np.array([10, -10, 5, -5, 0])
    if k % 512:
        return np.exp2(np.random.permutation(np.resize(levels, k // 32))).repeat(32)
    a = np.empty((k // 512, 16))
    for p in range(k // 512):
        a[p, :8] = np.random.permutation(np.resize(levels, 8))
        for g in range(8):
            far = levels[np.abs(levels - a[p, g]) >= 10]
            a[p, g + 8] = far[np.random.randint(len(far))]
    return np.exp2(a.ravel()).repeat(32)


def f64(x):
    return np.asarray(x).astype(np.float64)


def striped(idx):
    return np.tile(idx.reshape(-1, 16).T, (8, 1)).astype(np.uint16)


def unstriped(offs):
    return offs[:16].T.reshape(-1).astype(np.int64)


def pack_weight(w):
    k, n = w.shape
    w = f64(np.asarray(w, np.float32).astype(ml_dtypes.bfloat16)).reshape(k // 32, 32, n)
    amax = np.abs(w).max(1)
    byte = np.clip(np.where(amax > 0, np.frexp(amax)[1] - 1 + 127 - 7, 1), 1, 254)
    scaled = (w * np.exp2(127.0 - byte)[:, None, :]).reshape(k, n).astype(np.float32)
    words = np.ascontiguousarray(scaled.reshape(k // 512, 128, 4, n).transpose(0, 1, 3, 2)).astype(ml_dtypes.float8_e4m3fn).view(np.uint8)
    return words, np.ascontiguousarray(byte.astype(np.uint8).reshape(k // 512, 16, n))


def unpack_weight(words, scales):
    g, p, n, _ = words.shape
    vals = np.ascontiguousarray(words).view(ml_dtypes.float8_e4m3fn).astype(np.float64) * np.repeat(np.exp2(scales.astype(np.float64) - 127.0), 8, axis=1)[..., None]
    return vals.transpose(0, 1, 3, 2).reshape(g * 512, n)


K, T, S, N, U = 512, 4096, 1024, 128, 2048


def setup_inputs():
    n = np.random.standard_normal
    s = mx_kscale(K)[:, None]
    packed_xT = pack_weight(n((K, T)) * s)
    return {
        "x_words": packed_xT[0],
        "x_scales": packed_xT[1],
        "mem": n((N, U)).astype(np.float32),
        "w1": (n((K, N)) / np.sqrt(K) / s).astype(np.float32),
        "offs": striped(np.random.permutation(T)[:S]),
        "slot": striped(np.random.permutation(U)[:S]),
    }


def reference(x_words, x_scales, mem, w1, offs, slot):
    xq = unpack_weight(x_words, x_scales)[:, unstriped(offs)]
    y = mxq(f64(w1), 0, "e4m3").T @ xq
    out = f64(mem).copy()
    out[:, unstriped(slot)] = y
    return out

@@ -1,0 +1,69 @@
+import concourse.mybir as mybir
+
+K, T, S, N, U = 512, 4096, 1024, 128, 2048
+FLOPS = 2 * K * N * S
+
+F32 = mybir.dt.float32
+BF16 = mybir.dt.bfloat16
+I32 = mybir.dt.int32
+U32 = mybir.dt.uint32
+U16 = mybir.dt.uint16
+U8 = mybir.dt.uint8
+FP8X4 = mybir.dt.float8_e4m3fn_x4
+
+P = 128
+PACK = 4
+HALF = S // 2
+PER_COL = 16
+
+
+def tile_picked_kvput_none_p_kernel(tc, x_words, x_scales, mem, w1, offs, slot, out):
+    nc = tc.nc
+    with tc.tile_pool(name="held", bufs=1) as held, tc.psum_pool(name="psum", bufs=1) as psum:
+        offs_sb = held.tile([P, S // PER_COL], U16, name="offs_sb")
+        slot_sb = held.tile([P, S // PER_COL], U16, name="slot_sb")
+        all_words = held.tile([P, T], U32, name="all_words", align_bytes=64)
+        all_scales = held.tile([P, T], U8, name="all_scales", align_bytes=64)
+        cache = held.tile([P, U], F32, name="cache", align_bytes=64)
+        w_raw = held.tile([P, PACK, N], F32, name="w_raw", align_bytes=64)
+        w_grouped = held.tile([P, N, PACK], BF16, name="w_grouped", align_bytes=64)
+        w_codes = held.tile([P, N], U32, name="w_codes", align_bytes=64)
+        w_scales = held.tile([P, N], U8, name="w_scales", align_bytes=64)
+        picked_scales = held.tile([P, S], U8, name="picked_scales", align_bytes=64)
+
+        nc.vector.memset(all_scales[:].bitcast(I32), 0)
+        nc.sync.dma_start(offs_sb[:], offs)
+        nc.sync.dma_start(w_raw[:], w1.rearrange("(p j) n -> p j n", j=PACK))
+        scale_rows = x_scales[0].bitcast(I32)
+        for q in range(4):
+            nc.scalar.dma_start(all_scales[32 * q : 32 * q + 4, :].bitcast(I32), scale_rows[4 * q : 4 * q + 4, :])
+        nc.sync.dma_start(all_words[:].bitcast(I32), x_words[0].rearrange("p c r -> p (c r)").bitcast(I32))
+        nc.sync.dma_start(slot_sb[:], slot)
+        nc.sync.dma_start(cache[:], mem)
+
+        nc.vector.tensor_copy(w_grouped[:], w_raw[:].rearrange("p j n -> p n j"))
+        nc.vector.quantize_mx(out=w_codes[:].bitcast(FP8X4), scales=w_scales[:], in_=w_grouped[:].rearrange("p n j -> p (n j)"))
+        nc.vector.tensor_copy(picked_scales[:], all_scales[:].indirect(offs_sb[:]))
+
+        results = []
+        for h, width in ((0, 256), (1, 512)):
+            cols = slice(h * HALF // PER_COL, (h + 1) * HALF // PER_COL)
+            picked_words = held.tile([P, HALF], U32, name="picked_words%d" % h, align_bytes=64)
+            nc.vector.tensor_copy(picked_words[:], all_words[:].indirect(offs_sb[:, cols]))
+            y = held.tile([P, HALF], F32, name="y%d" % h, align_bytes=64)
+            for c in range(0, HALF, width):
+                acc = psum.tile([P, width], F32, name="acc%d_%d" % (h, c))
+                nc.tensor.matmul_mx(
+                    out=acc[:],
+                    lhsT=w_codes[:].bitcast(FP8X4),
+                    lhsT_scale=w_scales[:],
+                    rhs=picked_words[:, c : c + width].bitcast(FP8X4),
+                    rhs_scale=picked_scales[:, h * HALF + c : h * HALF + c + width],
+                    start=True,
+                    stop=True,
+                )
+                nc.scalar.copy(y[:, c : c + width], acc[:])
+            results.append((cols, y))
+        for cols, y in results:
+            nc.vector.tensor_copy(cache[:].indirect(slot_sb[:, cols]), y[:])
+        nc.sync.dma_start(out, cache[:])

@@ -23,32 +23,34 @@ def tile_picked_kvput_none_p_kernel(tc, x_words, x_scales, mem, w1, offs, slot, 
         offs_sb = held.tile([P, S // PER_COL], U16, name="offs_sb")
         slot_sb = held.tile([P, S // PER_COL], U16, name="slot_sb")
         all_words = held.tile([P, T], U32, name="all_words", align_bytes=64)
-        all_scales = held.tile([P, T], U8, name="all_scales", align_bytes=64)
+        all_scales = held.tile([P, T], U8, name="all_scales", tag="shared", align_bytes=64)
         cache = held.tile([P, U], F32, name="cache", align_bytes=64)
         w_raw = held.tile([P, PACK, N], F32, name="w_raw", align_bytes=64)
         w_grouped = held.tile([P, N, PACK], BF16, name="w_grouped", align_bytes=64)
         w_codes = held.tile([P, N], U32, name="w_codes", align_bytes=64)
         w_scales = held.tile([P, N], U8, name="w_scales", align_bytes=64)
         picked_scales = held.tile([P, S], U8, name="picked_scales", align_bytes=64)
+        plane = held.tile([P, S], U8, name="plane", align_bytes=64)
 
         nc.vector.memset(all_scales[:].bitcast(I32), 0)
         nc.sync.dma_start(offs_sb[:], offs)
         nc.sync.dma_start(w_raw[:], w1.rearrange("(p j) n -> p j n", j=PACK))
-        scale_rows = x_scales[0].bitcast(I32)
-        for q in range(4):
-            nc.scalar.dma_start(all_scales[32 * q : 32 * q + 4, :].bitcast(I32), scale_rows[4 * q : 4 * q + 4, :])
+        nc.vector.memset(plane[:].bitcast(I32), 0)
+        nc.scalar.dma_start(all_scales[0:P:8, :].bitcast(I32), x_scales[0].bitcast(I32))
         nc.sync.dma_start(all_words[:].bitcast(I32), x_words[0].rearrange("p c r -> p (c r)").bitcast(I32))
         nc.sync.dma_start(slot_sb[:], slot)
         nc.sync.dma_start(cache[:], mem)
 
-        nc.vector.tensor_copy(w_grouped[:], w_raw[:].rearrange("p j n -> p n j"))
-        nc.vector.quantize_mx(out=w_codes[:].bitcast(FP8X4), scales=w_scales[:], in_=w_grouped[:].rearrange("p n j -> p (n j)"))
+        nc.scalar.copy(w_grouped[:], w_raw[:].rearrange("p j n -> p n j"))
         nc.vector.tensor_copy(picked_scales[:], all_scales[:].indirect(offs_sb[:]))
+        for r in range(4):
+            nc.scalar.dma_start(plane[r:P:32, :].bitcast(I32), picked_scales[8 * r : P : 32, :].bitcast(I32))
+        nc.vector.quantize_mx(out=w_codes[:].bitcast(FP8X4), scales=w_scales[:], in_=w_grouped[:].rearrange("p n j -> p (n j)"))
 
         results = []
         for h, width in ((0, 256), (1, 512)):
             cols = slice(h * HALF // PER_COL, (h + 1) * HALF // PER_COL)
-            picked_words = held.tile([P, HALF], U32, name="picked_words%d" % h, align_bytes=64)
+            picked_words = held.tile([P, HALF], U32, name="picked_words%d" % h, tag=("shared", "second")[h], align_bytes=64)
             nc.vector.tensor_copy(picked_words[:], all_words[:].indirect(offs_sb[:, cols]))
             y = held.tile([P, HALF], F32, name="y%d" % h, align_bytes=64)
             for c in range(0, HALF, width):
@@ -58,7 +60,7 @@ def tile_picked_kvput_none_p_kernel(tc, x_words, x_scales, mem, w1, offs, slot, 
                     lhsT=w_codes[:].bitcast(FP8X4),
                     lhsT_scale=w_scales[:],
                     rhs=picked_words[:, c : c + width].bitcast(FP8X4),
-                    rhs_scale=picked_scales[:, h * HALF + c : h * HALF + c + width],
+                    rhs_scale=plane[:, h * HALF + c : h * HALF + c + width],
                     start=True,
                     stop=True,
                 )

@@ -15,6 +15,7 @@ P = 128
 PACK = 4
 HALF = S // 2
 PER_COL = 16
+PIECE = 256
 
 
 def tile_picked_kvput_none_p_kernel(tc, x_words, x_scales, mem, w1, offs, slot, out):
@@ -24,7 +25,6 @@ def tile_picked_kvput_none_p_kernel(tc, x_words, x_scales, mem, w1, offs, slot, 
         slot_sb = held.tile([P, S // PER_COL], U16, name="slot_sb")
         all_words = held.tile([P, T], U32, name="all_words", align_bytes=64)
         all_scales = held.tile([P, T], U8, name="all_scales", tag="shared", align_bytes=64)
-        cache = held.tile([P, U], F32, name="cache", align_bytes=64)
         w_raw = held.tile([P, PACK, N], F32, name="w_raw", align_bytes=64)
         w_grouped = held.tile([P, N, PACK], BF16, name="w_grouped", align_bytes=64)
         w_codes = held.tile([P, N], U32, name="w_codes", align_bytes=64)
@@ -32,40 +32,40 @@ def tile_picked_kvput_none_p_kernel(tc, x_words, x_scales, mem, w1, offs, slot, 
         picked_scales = held.tile([P, S], U8, name="picked_scales", align_bytes=64)
         plane = held.tile([P, S], U8, name="plane", align_bytes=64)
 
-        nc.vector.memset(all_scales[:].bitcast(I32), 0)
+        nc.vector.memset(all_scales[0:112, :].bitcast(I32), 0)
         nc.sync.dma_start(offs_sb[:], offs)
+        nc.sync.dma_start(all_scales[112:P, :].bitcast(I32), x_scales[0].bitcast(I32))
         nc.sync.dma_start(w_raw[:], w1.rearrange("(p j) n -> p j n", j=PACK))
         nc.vector.memset(plane[:].bitcast(I32), 0)
-        nc.scalar.dma_start(all_scales[0:P:8, :].bitcast(I32), x_scales[0].bitcast(I32))
         nc.sync.dma_start(all_words[:].bitcast(I32), x_words[0].rearrange("p c r -> p (c r)").bitcast(I32))
         nc.sync.dma_start(slot_sb[:], slot)
-        nc.sync.dma_start(cache[:], mem)
 
         nc.scalar.copy(w_grouped[:], w_raw[:].rearrange("p j n -> p n j"))
         nc.vector.tensor_copy(picked_scales[:], all_scales[:].indirect(offs_sb[:]))
-        for r in range(4):
-            nc.scalar.dma_start(plane[r:P:32, :].bitcast(I32), picked_scales[8 * r : P : 32, :].bitcast(I32))
+        for q in range(4):
+            nc.sync.dma_start(plane[32 * q : 32 * q + 4, :].bitcast(I32), picked_scales[112 + 4 * q : 116 + 4 * q, :].bitcast(I32))
+        cache = held.tile([P, U], F32, name="cache", tag="shared", align_bytes=64)
+        nc.sync.dma_start(cache[:], mem)
         nc.vector.quantize_mx(out=w_codes[:].bitcast(FP8X4), scales=w_scales[:], in_=w_grouped[:].rearrange("p n j -> p (n j)"))
 
-        results = []
-        for h, width in ((0, 256), (1, 512)):
-            cols = slice(h * HALF // PER_COL, (h + 1) * HALF // PER_COL)
-            picked_words = held.tile([P, HALF], U32, name="picked_words%d" % h, tag=("shared", "second")[h], align_bytes=64)
-            nc.vector.tensor_copy(picked_words[:], all_words[:].indirect(offs_sb[:, cols]))
-            y = held.tile([P, HALF], F32, name="y%d" % h, align_bytes=64)
-            for c in range(0, HALF, width):
-                acc = psum.tile([P, width], F32, name="acc%d_%d" % (h, c))
+        y_first = held.tile([P, PIECE], F32, name="y_first", align_bytes=64)
+        y_rest = held.tile([P, S - PIECE], F32, name="y_rest", align_bytes=64)
+        for h in range(2):
+            picked_words = held.tile([P, HALF], U32, name="picked_words%d" % h, align_bytes=64)
+            nc.vector.tensor_copy(picked_words[:], all_words[:].indirect(offs_sb[:, h * HALF // PER_COL : (h + 1) * HALF // PER_COL]))
+            for c in range(0, HALF, PIECE):
+                j = h * HALF + c
+                acc = psum.tile([P, PIECE], F32, name="acc%d" % j)
                 nc.tensor.matmul_mx(
                     out=acc[:],
                     lhsT=w_codes[:].bitcast(FP8X4),
                     lhsT_scale=w_scales[:],
-                    rhs=picked_words[:, c : c + width].bitcast(FP8X4),
-                    rhs_scale=plane[:, h * HALF + c : h * HALF + c + width],
+                    rhs=picked_words[:, c : c + PIECE].bitcast(FP8X4),
+                    rhs_scale=plane[:, j : j + PIECE],
                     start=True,
                     stop=True,
                 )
-                nc.scalar.copy(y[:, c : c + width], acc[:])
-            results.append((cols, y))
-        for cols, y in results:
-            nc.vector.tensor_copy(cache[:].indirect(slot_sb[:, cols]), y[:])
+                nc.scalar.copy(y_first[:] if j == 0 else y_rest[:, j - PIECE : j], acc[:])
+        nc.vector.tensor_copy(cache[:].indirect(slot_sb[:, 0 : PIECE // PER_COL]), y_first[:])
+        nc.vector.tensor_copy(cache[:].indirect(slot_sb[:, PIECE // PER_COL : S // PER_COL]), y_rest[:])
         nc.sync.dma_start(out, cache[:])

@@ -34,7 +34,7 @@ def tile_picked_kvput_none_p_kernel(tc, x_words, x_scales, mem, w1, offs, slot, 
 
         nc.vector.memset(all_scales[0:112, :].bitcast(I32), 0)
         nc.sync.dma_start(offs_sb[:], offs)
-        nc.sync.dma_start(all_scales[112:P, :].bitcast(I32), x_scales[0].bitcast(I32))
+        nc.scalar.dma_start(all_scales[112:P, :].bitcast(I32), x_scales[0].bitcast(I32))
         nc.sync.dma_start(w_raw[:], w1.rearrange("(p j) n -> p j n", j=PACK))
         nc.vector.memset(plane[:].bitcast(I32), 0)
         nc.sync.dma_start(all_words[:].bitcast(I32), x_words[0].rearrange("p c r -> p (c r)").bitcast(I32))

@@ -16,6 +16,7 @@ PACK = 4
 HALF = S // 2
 PER_COL = 16
 PIECE = 256
+LEAD = 512
 
 
 def tile_picked_kvput_none_p_kernel(tc, x_words, x_scales, mem, w1, offs, slot, out):
@@ -24,29 +25,35 @@ def tile_picked_kvput_none_p_kernel(tc, x_words, x_scales, mem, w1, offs, slot, 
         offs_sb = held.tile([P, S // PER_COL], U16, name="offs_sb")
         slot_sb = held.tile([P, S // PER_COL], U16, name="slot_sb")
         all_words = held.tile([P, T], U32, name="all_words", align_bytes=64)
-        all_scales = held.tile([P, T], U8, name="all_scales", tag="shared", align_bytes=64)
+        all_scales = held.tile([P, T], U8, name="all_scales", align_bytes=64)
         w_raw = held.tile([P, PACK, N], F32, name="w_raw", align_bytes=64)
-        w_grouped = held.tile([P, N, PACK], BF16, name="w_grouped", align_bytes=64)
+        w_grouped = held.tile([P, N, PACK], BF16, name="w_grouped", tag="shared", align_bytes=64)
         w_codes = held.tile([P, N], U32, name="w_codes", align_bytes=64)
         w_scales = held.tile([P, N], U8, name="w_scales", align_bytes=64)
-        picked_scales = held.tile([P, S], U8, name="picked_scales", align_bytes=64)
+        picked_scales = [held.tile([P, HALF], U8, name="picked_scales%d" % h, align_bytes=64) for h in range(2)]
         plane = held.tile([P, S], U8, name="plane", align_bytes=64)
+        words_hbm = x_words[0].rearrange("p c r -> p (c r)").bitcast(I32)
 
-        nc.vector.memset(all_scales[0:112, :].bitcast(I32), 0)
-        nc.sync.dma_start(offs_sb[:], offs)
-        nc.scalar.dma_start(all_scales[112:P, :].bitcast(I32), x_scales[0].bitcast(I32))
-        nc.sync.dma_start(w_raw[:], w1.rearrange("(p j) n -> p j n", j=PACK))
+        nc.vector.memset(all_scales[:].bitcast(I32), 0)
         nc.vector.memset(plane[:].bitcast(I32), 0)
-        nc.sync.dma_start(all_words[:].bitcast(I32), x_words[0].rearrange("p c r -> p (c r)").bitcast(I32))
+        nc.sync.dma_start(w_raw[:], w1.rearrange("(p j) n -> p j n", j=PACK))
+        nc.sync.dma_start(offs_sb[:], offs)
+        nc.sync.dma_start(all_words[:, 0:LEAD].bitcast(I32), words_hbm[:, 0:LEAD])
+        nc.sync.dma_start(all_scales[32:96:4, :].bitcast(I32), x_scales[0].bitcast(I32))
+        nc.sync.dma_start(all_words[:, LEAD:T].bitcast(I32), words_hbm[:, LEAD:T])
         nc.sync.dma_start(slot_sb[:], slot)
 
+        def pick_scales(h):
+            nc.vector.tensor_copy(picked_scales[h][:], all_scales[:].indirect(offs_sb[:, h * HALF // PER_COL : (h + 1) * HALF // PER_COL]))
+            for q in range(4):
+                nc.sync.dma_start(plane[32 * q : 32 * q + 4, h * HALF : (h + 1) * HALF].bitcast(I32), picked_scales[h][32 + 16 * q : 48 + 16 * q : 4, :].bitcast(I32))
+
         nc.scalar.copy(w_grouped[:], w_raw[:].rearrange("p j n -> p n j"))
-        nc.vector.tensor_copy(picked_scales[:], all_scales[:].indirect(offs_sb[:]))
-        for q in range(4):
-            nc.sync.dma_start(plane[32 * q : 32 * q + 4, :].bitcast(I32), picked_scales[112 + 4 * q : 116 + 4 * q, :].bitcast(I32))
+        pick_scales(0)
+        nc.vector.quantize_mx(out=w_codes[:].bitcast(FP8X4), scales=w_scales[:], in_=w_grouped[:].rearrange("p n j -> p (n j)"))
         cache = held.tile([P, U], F32, name="cache", tag="shared", align_bytes=64)
         nc.sync.dma_start(cache[:], mem)
-        nc.vector.quantize_mx(out=w_codes[:].bitcast(FP8X4), scales=w_scales[:], in_=w_grouped[:].rearrange("p n j -> p (n j)"))
+        pick_scales(1)
 
         y_first = held.tile([P, PIECE], F32, name="y_first", align_bytes=64)
         y_rest = held.tile([P, S - PIECE], F32, name="y_rest", align_bytes=64)

@@ -15,8 +15,9 @@ P = 128
 PACK = 4
 HALF = S // 2
 PER_COL = 16
-PIECE = 256
-LEAD = 512
+LEAD = 768
+FIRST = 256
+WIDTHS = ((128, 128, 256), (256, 256))
 
 
 def tile_picked_kvput_none_p_kernel(tc, x_words, x_scales, mem, w1, offs, slot, out):
@@ -55,24 +56,27 @@ def tile_picked_kvput_none_p_kernel(tc, x_words, x_scales, mem, w1, offs, slot, 
         nc.sync.dma_start(cache[:], mem)
         pick_scales(1)
 
-        y_first = held.tile([P, PIECE], F32, name="y_first", align_bytes=64)
-        y_rest = held.tile([P, S - PIECE], F32, name="y_rest", align_bytes=64)
+        y_first = held.tile([P, FIRST], F32, name="y_first", align_bytes=64)
+        y_rest = held.tile([P, S - FIRST], F32, name="y_rest", align_bytes=64)
+        j = 0
         for h in range(2):
             picked_words = held.tile([P, HALF], U32, name="picked_words%d" % h, align_bytes=64)
             nc.vector.tensor_copy(picked_words[:], all_words[:].indirect(offs_sb[:, h * HALF // PER_COL : (h + 1) * HALF // PER_COL]))
-            for c in range(0, HALF, PIECE):
-                j = h * HALF + c
-                acc = psum.tile([P, PIECE], F32, name="acc%d" % j)
+            c = 0
+            for width in WIDTHS[h]:
+                acc = psum.tile([P, width], F32, name="acc%d" % j)
                 nc.tensor.matmul_mx(
                     out=acc[:],
                     lhsT=w_codes[:].bitcast(FP8X4),
                     lhsT_scale=w_scales[:],
-                    rhs=picked_words[:, c : c + PIECE].bitcast(FP8X4),
-                    rhs_scale=plane[:, j : j + PIECE],
+                    rhs=picked_words[:, c : c + width].bitcast(FP8X4),
+                    rhs_scale=plane[:, j : j + width],
                     start=True,
                     stop=True,
                 )
-                nc.scalar.copy(y_first[:] if j == 0 else y_rest[:, j - PIECE : j], acc[:])
-        nc.vector.tensor_copy(cache[:].indirect(slot_sb[:, 0 : PIECE // PER_COL]), y_first[:])
-        nc.vector.tensor_copy(cache[:].indirect(slot_sb[:, PIECE // PER_COL : S // PER_COL]), y_rest[:])
+                nc.scalar.copy(y_first[:, j : j + width] if j < FIRST else y_rest[:, j - FIRST : j - FIRST + width], acc[:])
+                c = c + width
+                j = j + width
+        nc.vector.tensor_copy(cache[:].indirect(slot_sb[:, 0 : FIRST // PER_COL]), y_first[:])
+        nc.vector.tensor_copy(cache[:].indirect(slot_sb[:, FIRST // PER_COL : S // PER_COL]), y_rest[:])
         nc.sync.dma_start(out, cache[:])

@@ -15,7 +15,6 @@ P = 128
 PACK = 4
 HALF = S // 2
 PER_COL = 16
-LEAD = 768
 FIRST = 256
 WIDTHS = ((128, 128, 256), (256, 256))
 
@@ -26,41 +25,43 @@ def tile_picked_kvput_none_p_kernel(tc, x_words, x_scales, mem, w1, offs, slot, 
         offs_sb = held.tile([P, S // PER_COL], U16, name="offs_sb")
         slot_sb = held.tile([P, S // PER_COL], U16, name="slot_sb")
         all_words = held.tile([P, T], U32, name="all_words", align_bytes=64)
-        all_scales = held.tile([P, T], U8, name="all_scales", align_bytes=64)
+        all_scales = held.tile([P, T], U8, name="all_scales", tag="scales_then_cache", align_bytes=64)
         w_raw = held.tile([P, PACK, N], F32, name="w_raw", align_bytes=64)
-        w_grouped = held.tile([P, N, PACK], BF16, name="w_grouped", tag="shared", align_bytes=64)
+        w_grouped = held.tile([P, N, PACK], BF16, name="w_grouped", tag="weights_then_words", align_bytes=64)
         w_codes = held.tile([P, N], U32, name="w_codes", align_bytes=64)
         w_scales = held.tile([P, N], U8, name="w_scales", align_bytes=64)
         picked_scales = [held.tile([P, HALF], U8, name="picked_scales%d" % h, align_bytes=64) for h in range(2)]
         plane = held.tile([P, S], U8, name="plane", align_bytes=64)
-        words_hbm = x_words[0].rearrange("p c r -> p (c r)").bitcast(I32)
 
-        nc.vector.memset(all_scales[:].bitcast(I32), 0)
+        nc.vector.memset(all_scales[0:112, :].bitcast(I32), 0)
         nc.vector.memset(plane[:].bitcast(I32), 0)
-        nc.sync.dma_start(w_raw[:], w1.rearrange("(p j) n -> p j n", j=PACK))
         nc.sync.dma_start(offs_sb[:], offs)
-        nc.sync.dma_start(all_words[:, 0:LEAD].bitcast(I32), words_hbm[:, 0:LEAD])
-        nc.sync.dma_start(all_scales[32:96:4, :].bitcast(I32), x_scales[0].bitcast(I32))
-        nc.sync.dma_start(all_words[:, LEAD:T].bitcast(I32), words_hbm[:, LEAD:T])
+        nc.scalar.dma_start(all_scales[112:P, :].bitcast(I32), x_scales[0].bitcast(I32))
+        nc.sync.dma_start(all_words[:].bitcast(I32), x_words[0].rearrange("p c r -> p (c r)").bitcast(I32))
+        nc.sync.dma_start(w_raw[:], w1.rearrange("(p j) n -> p j n", j=PACK))
         nc.sync.dma_start(slot_sb[:], slot)
 
-        def pick_scales(h):
+        def gather_scales(h):
             nc.vector.tensor_copy(picked_scales[h][:], all_scales[:].indirect(offs_sb[:, h * HALF // PER_COL : (h + 1) * HALF // PER_COL]))
-            for q in range(4):
-                nc.sync.dma_start(plane[32 * q : 32 * q + 4, h * HALF : (h + 1) * HALF].bitcast(I32), picked_scales[h][32 + 16 * q : 48 + 16 * q : 4, :].bitcast(I32))
 
-        nc.scalar.copy(w_grouped[:], w_raw[:].rearrange("p j n -> p n j"))
-        pick_scales(0)
-        nc.vector.quantize_mx(out=w_codes[:].bitcast(FP8X4), scales=w_scales[:], in_=w_grouped[:].rearrange("p n j -> p (n j)"))
-        cache = held.tile([P, U], F32, name="cache", tag="shared", align_bytes=64)
+        def move_scales(h):
+            for q in range(4):
+                nc.sync.dma_start(plane[32 * q : 32 * q + 4, h * HALF : (h + 1) * HALF].bitcast(I32), picked_scales[h][112 + 4 * q : 116 + 4 * q, :].bitcast(I32))
+
+        gather_scales(0)
+        move_scales(0)
+        gather_scales(1)
+        cache = held.tile([P, U], F32, name="cache", tag="scales_then_cache", align_bytes=64)
         nc.sync.dma_start(cache[:], mem)
-        pick_scales(1)
+        move_scales(1)
+        nc.scalar.copy(w_grouped[:], w_raw[:].rearrange("p j n -> p n j"))
+        nc.vector.quantize_mx(out=w_codes[:].bitcast(FP8X4), scales=w_scales[:], in_=w_grouped[:].rearrange("p n j -> p (n j)"))
 
         y_first = held.tile([P, FIRST], F32, name="y_first", align_bytes=64)
         y_rest = held.tile([P, S - FIRST], F32, name="y_rest", align_bytes=64)
         j = 0
         for h in range(2):
-            picked_words = held.tile([P, HALF], U32, name="picked_words%d" % h, align_bytes=64)
+            picked_words = held.tile([P, HALF], U32, name="picked_words%d" % h, tag="weights_then_words" if h else "first_words", align_bytes=64)
             nc.vector.tensor_copy(picked_words[:], all_words[:].indirect(offs_sb[:, h * HALF // PER_COL : (h + 1) * HALF // PER_COL]))
             c = 0
             for width in WIDTHS[h]:

@@ -26,8 +26,8 @@ def tile_picked_kvput_none_p_kernel(tc, x_words, x_scales, mem, w1, offs, slot, 
         slot_sb = held.tile([P, S // PER_COL], U16, name="slot_sb")
         all_words = held.tile([P, T], U32, name="all_words", align_bytes=64)
         all_scales = held.tile([P, T], U8, name="all_scales", tag="scales_then_cache", align_bytes=64)
-        w_raw = held.tile([P, PACK, N], F32, name="w_raw", align_bytes=64)
-        w_grouped = held.tile([P, N, PACK], BF16, name="w_grouped", tag="weights_then_words", align_bytes=64)
+        w_raw = held.tile([P, PACK, N], F32, name="w_raw", tag="weights_then_words", align_bytes=64)
+        w_grouped = held.tile([P, N, PACK], BF16, name="w_grouped", align_bytes=64)
         w_codes = held.tile([P, N], U32, name="w_codes", align_bytes=64)
         w_scales = held.tile([P, N], U8, name="w_scales", align_bytes=64)
         picked_scales = [held.tile([P, HALF], U8, name="picked_scales%d" % h, align_bytes=64) for h in range(2)]

@@ -16,7 +16,7 @@ PACK = 4
 HALF = S // 2
 PER_COL = 16
 FIRST = 256
-WIDTHS = ((128, 128, 256), (256, 256))
+WIDTHS = ((128, 128, 256), (256, 128, 128))
 
 
 def tile_picked_kvput_none_p_kernel(tc, x_words, x_scales, mem, w1, offs, slot, out):
@@ -54,7 +54,7 @@ def tile_picked_kvput_none_p_kernel(tc, x_words, x_scales, mem, w1, offs, slot, 
         cache = held.tile([P, U], F32, name="cache", tag="scales_then_cache", align_bytes=64)
         nc.sync.dma_start(cache[:], mem)
         move_scales(1)
-        nc.scalar.copy(w_grouped[:], w_raw[:].rearrange("p j n -> p n j"))
+        nc.scalar.copy(w_grouped[:].rearrange("p (c i) j -> p c j i", i=4), w_raw[:].rearrange("p j (c i) -> p c j i", i=4))
         nc.vector.quantize_mx(out=w_codes[:].bitcast(FP8X4), scales=w_scales[:], in_=w_grouped[:].rearrange("p n j -> p (n j)"))
 
         y_first = held.tile([P, FIRST], F32, name="y_first", align_bytes=64)

@@ -27,7 +27,7 @@ def tile_picked_kvput_none_p_kernel(tc, x_words, x_scales, mem, w1, offs, slot, 
         all_words = held.tile([P, T], U32, name="all_words", align_bytes=64)
         all_scales = held.tile([P, T], U8, name="all_scales", tag="scales_then_cache", align_bytes=64)
         w_raw = held.tile([P, PACK, N], F32, name="w_raw", tag="weights_then_words", align_bytes=64)
-        w_grouped = held.tile([P, N, PACK], BF16, name="w_grouped", align_bytes=64)
+        w_grouped = [held.tile([P, N // 2, PACK], BF16, name="w_grouped%d" % u, align_bytes=64) for u in range(2)]
         w_codes = held.tile([P, N], U32, name="w_codes", align_bytes=64)
         w_scales = held.tile([P, N], U8, name="w_scales", align_bytes=64)
         picked_scales = [held.tile([P, HALF], U8, name="picked_scales%d" % h, align_bytes=64) for h in range(2)]
@@ -54,8 +54,10 @@ def tile_picked_kvput_none_p_kernel(tc, x_words, x_scales, mem, w1, offs, slot, 
         cache = held.tile([P, U], F32, name="cache", tag="scales_then_cache", align_bytes=64)
         nc.sync.dma_start(cache[:], mem)
         move_scales(1)
-        nc.scalar.copy(w_grouped[:].rearrange("p (c i) j -> p c j i", i=4), w_raw[:].rearrange("p j (c i) -> p c j i", i=4))
-        nc.vector.quantize_mx(out=w_codes[:].bitcast(FP8X4), scales=w_scales[:], in_=w_grouped[:].rearrange("p n j -> p (n j)"))
+        for u in range(2):
+            cols = slice(u * N // 2, (u + 1) * N // 2)
+            nc.scalar.copy(w_grouped[u][:].rearrange("p (c i) j -> p c j i", i=4), w_raw[:, :, cols].rearrange("p j (c i) -> p c j i", i=4))
+            nc.vector.quantize_mx(out=w_codes[:, cols].bitcast(FP8X4), scales=w_scales[:, cols], in_=w_grouped[u][:].rearrange("p n j -> p (n j)"))
 
         y_first = held.tile([P, FIRST], F32, name="y_first", align_bytes=64)
         y_rest = held.tile([P, S - FIRST], F32, name="y_rest", align_bytes=64)

@@ -17,6 +17,7 @@ HALF = S // 2
 PER_COL = 16
 FIRST = 256
 WIDTHS = ((128, 128, 256), (256, 128, 128))
+PIECE = 4096
 
 
 def tile_picked_kvput_none_p_kernel(tc, x_words, x_scales, mem, w1, offs, slot, out):
@@ -25,35 +26,27 @@ def tile_picked_kvput_none_p_kernel(tc, x_words, x_scales, mem, w1, offs, slot, 
         offs_sb = held.tile([P, S // PER_COL], U16, name="offs_sb")
         slot_sb = held.tile([P, S // PER_COL], U16, name="slot_sb")
         all_words = held.tile([P, T], U32, name="all_words", align_bytes=64)
-        all_scales = held.tile([P, T], U8, name="all_scales", tag="scales_then_cache", align_bytes=64)
+        all_scales = held.tile([P, T], U8, name="all_scales", tag="scales_then_words", align_bytes=64)
+        cache = held.tile([P, U], F32, name="cache", align_bytes=64)
         w_raw = held.tile([P, PACK, N], F32, name="w_raw", tag="weights_then_words", align_bytes=64)
         w_grouped = [held.tile([P, N // 2, PACK], BF16, name="w_grouped%d" % u, align_bytes=64) for u in range(2)]
         w_codes = held.tile([P, N], U32, name="w_codes", align_bytes=64)
         w_scales = held.tile([P, N], U8, name="w_scales", align_bytes=64)
-        picked_scales = [held.tile([P, HALF], U8, name="picked_scales%d" % h, align_bytes=64) for h in range(2)]
+        picked_scales = held.tile([P, S], U8, name="picked_scales", align_bytes=64)
         plane = held.tile([P, S], U8, name="plane", align_bytes=64)
 
         nc.vector.memset(all_scales[0:112, :].bitcast(I32), 0)
         nc.vector.memset(plane[:].bitcast(I32), 0)
         nc.sync.dma_start(offs_sb[:], offs)
-        nc.scalar.dma_start(all_scales[112:P, :].bitcast(I32), x_scales[0].bitcast(I32))
-        nc.sync.dma_start(all_words[:].bitcast(I32), x_words[0].rearrange("p c r -> p (c r)").bitcast(I32))
-        nc.sync.dma_start(w_raw[:], w1.rearrange("(p j) n -> p j n", j=PACK))
+        nc.sync.dma_start(all_scales[112:P, :].bitcast(I32), x_scales[0].bitcast(I32))
         nc.sync.dma_start(slot_sb[:], slot)
+        nc.scalar.dma_start(all_words[:].bitcast(I32), x_words[0].rearrange("p c r -> p (c r)").bitcast(I32), max_dma_last_dim=PIECE)
+        nc.scalar.dma_start(w_raw[:], w1.rearrange("(p j) n -> p j n", j=PACK))
+        nc.scalar.dma_start(cache[:], mem, max_dma_last_dim=PIECE)
 
-        def gather_scales(h):
-            nc.vector.tensor_copy(picked_scales[h][:], all_scales[:].indirect(offs_sb[:, h * HALF // PER_COL : (h + 1) * HALF // PER_COL]))
-
-        def move_scales(h):
-            for q in range(4):
-                nc.sync.dma_start(plane[32 * q : 32 * q + 4, h * HALF : (h + 1) * HALF].bitcast(I32), picked_scales[h][112 + 4 * q : 116 + 4 * q, :].bitcast(I32))
-
-        gather_scales(0)
-        move_scales(0)
-        gather_scales(1)
-        cache = held.tile([P, U], F32, name="cache", tag="scales_then_cache", align_bytes=64)
-        nc.sync.dma_start(cache[:], mem)
-        move_scales(1)
+        nc.vector.tensor_copy(picked_scales[:], all_scales[:].indirect(offs_sb[:]))
+        for q in range(4):
+            nc.sync.dma_start(plane[32 * q : 32 * q + 4, :].bitcast(I32), picked_scales[112 + 4 * q : 116 + 4 * q, :].bitcast(I32))
         for u in range(2):
             cols = slice(u * N // 2, (u + 1) * N // 2)
             nc.scalar.copy(w_grouped[u][:].rearrange("p (c i) j -> p c j i", i=4), w_raw[:, :, cols].rearrange("p j (c i) -> p c j i", i=4))
@@ -63,7 +56,7 @@ def tile_picked_kvput_none_p_kernel(tc, x_words, x_scales, mem, w1, offs, slot, 
         y_rest = held.tile([P, S - FIRST], F32, name="y_rest", align_bytes=64)
         j = 0
         for h in range(2):
-            picked_words = held.tile([P, HALF], U32, name="picked_words%d" % h, tag="weights_then_words" if h else "first_words", align_bytes=64)
+            picked_words = held.tile([P, HALF], U32, name="picked_words%d" % h, tag="weights_then_words" if h else "scales_then_words", align_bytes=64)
             nc.vector.tensor_copy(picked_words[:], all_words[:].indirect(offs_sb[:, h * HALF // PER_COL : (h + 1) * HALF // PER_COL]))
             c = 0
             for width in WIDTHS[h]:

@@ -17,7 +17,6 @@ HALF = S // 2
 PER_COL = 16
 FIRST = 256
 WIDTHS = ((128, 128, 256), (256, 128, 128))
-PIECE = 4096
 
 
 def tile_picked_kvput_none_p_kernel(tc, x_words, x_scales, mem, w1, offs, slot, out):
@@ -26,8 +25,7 @@ def tile_picked_kvput_none_p_kernel(tc, x_words, x_scales, mem, w1, offs, slot, 
         offs_sb = held.tile([P, S // PER_COL], U16, name="offs_sb")
         slot_sb = held.tile([P, S // PER_COL], U16, name="slot_sb")
         all_words = held.tile([P, T], U32, name="all_words", align_bytes=64)
-        all_scales = held.tile([P, T], U8, name="all_scales", tag="scales_then_words", align_bytes=64)
-        cache = held.tile([P, U], F32, name="cache", align_bytes=64)
+        all_scales = held.tile([P, T], U8, name="all_scales", tag="scales_then_cache", align_bytes=64)
         w_raw = held.tile([P, PACK, N], F32, name="w_raw", tag="weights_then_words", align_bytes=64)
         w_grouped = [held.tile([P, N // 2, PACK], BF16, name="w_grouped%d" % u, align_bytes=64) for u in range(2)]
         w_codes = held.tile([P, N], U32, name="w_codes", align_bytes=64)
@@ -38,15 +36,16 @@ def tile_picked_kvput_none_p_kernel(tc, x_words, x_scales, mem, w1, offs, slot, 
         nc.vector.memset(all_scales[0:112, :].bitcast(I32), 0)
         nc.vector.memset(plane[:].bitcast(I32), 0)
         nc.sync.dma_start(offs_sb[:], offs)
-        nc.sync.dma_start(all_scales[112:P, :].bitcast(I32), x_scales[0].bitcast(I32))
+        nc.scalar.dma_start(all_scales[112:P, :].bitcast(I32), x_scales[0].bitcast(I32))
         nc.sync.dma_start(slot_sb[:], slot)
-        nc.scalar.dma_start(all_words[:].bitcast(I32), x_words[0].rearrange("p c r -> p (c r)").bitcast(I32), max_dma_last_dim=PIECE)
+        nc.scalar.dma_start(all_words[:].bitcast(I32), x_words[0].rearrange("p c r -> p (c r)").bitcast(I32))
         nc.scalar.dma_start(w_raw[:], w1.rearrange("(p j) n -> p j n", j=PACK))
-        nc.scalar.dma_start(cache[:], mem, max_dma_last_dim=PIECE)
 
         nc.vector.tensor_copy(picked_scales[:], all_scales[:].indirect(offs_sb[:]))
         for q in range(4):
             nc.sync.dma_start(plane[32 * q : 32 * q + 4, :].bitcast(I32), picked_scales[112 + 4 * q : 116 + 4 * q, :].bitcast(I32))
+        cache = held.tile([P, U], F32, name="cache", tag="scales_then_cache", align_bytes=64)
+        nc.sync.dma_start(cache[:], mem)
         for u in range(2):
             cols = slice(u * N // 2, (u + 1) * N // 2)
             nc.scalar.copy(w_grouped[u][:].rearrange("p (c i) j -> p c j i", i=4), w_raw[:, :, cols].rearrange("p j (c i) -> p c j i", i=4))
@@ -56,7 +55,7 @@ def tile_picked_kvput_none_p_kernel(tc, x_words, x_scales, mem, w1, offs, slot, 
         y_rest = held.tile([P, S - FIRST], F32, name="y_rest", align_bytes=64)
         j = 0
         for h in range(2):
-            picked_words = held.tile([P, HALF], U32, name="picked_words%d" % h, tag="weights_then_words" if h else "scales_then_words", align_bytes=64)
+            picked_words = held.tile([P, HALF], U32, name="picked_words%d" % h, tag="weights_then_words" if h else "first_words", align_bytes=64)
             nc.vector.tensor_copy(picked_words[:], all_words[:].indirect(offs_sb[:, h * HALF // PER_COL : (h + 1) * HALF // PER_COL]))
             c = 0
             for width in WIDTHS[h]:

@@ -30,22 +30,30 @@ def tile_picked_kvput_none_p_kernel(tc, x_words, x_scales, mem, w1, offs, slot, 
         w_grouped = [held.tile([P, N // 2, PACK], BF16, name="w_grouped%d" % u, align_bytes=64) for u in range(2)]
         w_codes = held.tile([P, N], U32, name="w_codes", align_bytes=64)
         w_scales = held.tile([P, N], U8, name="w_scales", align_bytes=64)
-        picked_scales = held.tile([P, S], U8, name="picked_scales", align_bytes=64)
+        picked_scales = [held.tile([P, HALF], U8, name="picked_scales%d" % h, align_bytes=64) for h in range(2)]
         plane = held.tile([P, S], U8, name="plane", align_bytes=64)
 
         nc.vector.memset(all_scales[0:112, :].bitcast(I32), 0)
         nc.vector.memset(plane[:].bitcast(I32), 0)
         nc.sync.dma_start(offs_sb[:], offs)
-        nc.scalar.dma_start(all_scales[112:P, :].bitcast(I32), x_scales[0].bitcast(I32))
         nc.sync.dma_start(slot_sb[:], slot)
+        nc.scalar.dma_start(all_scales[112:P, :].bitcast(I32), x_scales[0].bitcast(I32))
         nc.scalar.dma_start(all_words[:].bitcast(I32), x_words[0].rearrange("p c r -> p (c r)").bitcast(I32))
         nc.scalar.dma_start(w_raw[:], w1.rearrange("(p j) n -> p j n", j=PACK))
 
-        nc.vector.tensor_copy(picked_scales[:], all_scales[:].indirect(offs_sb[:]))
-        for q in range(4):
-            nc.sync.dma_start(plane[32 * q : 32 * q + 4, :].bitcast(I32), picked_scales[112 + 4 * q : 116 + 4 * q, :].bitcast(I32))
+        def gather_scales(h):
+            nc.vector.tensor_copy(picked_scales[h][:], all_scales[:].indirect(offs_sb[:, h * HALF // PER_COL : (h + 1) * HALF // PER_COL]))
+
+        def move_scales(h):
+            for q in range(4):
+                nc.sync.dma_start(plane[32 * q : 32 * q + 4, h * HALF : (h + 1) * HALF].bitcast(I32), picked_scales[h][112 + 4 * q : 116 + 4 * q, :].bitcast(I32))
+
+        gather_scales(0)
+        move_scales(0)
+        gather_scales(1)
         cache = held.tile([P, U], F32, name="cache", tag="scales_then_cache", align_bytes=64)
         nc.sync.dma_start(cache[:], mem)
+        move_scales(1)
         for u in range(2):
             cols = slice(u * N // 2, (u + 1) * N // 2)
             nc.scalar.copy(w_grouped[u][:].rearrange("p (c i) j -> p c j i", i=4), w_raw[:, :, cols].rearrange("p j (c i) -> p c j i", i=4))

@@ -26,6 +26,7 @@ def tile_picked_kvput_none_p_kernel(tc, x_words, x_scales, mem, w1, offs, slot, 
         slot_sb = held.tile([P, S // PER_COL], U16, name="slot_sb")
         all_words = held.tile([P, T], U32, name="all_words", align_bytes=64)
         all_scales = held.tile([P, T], U8, name="all_scales", tag="scales_then_cache", align_bytes=64)
+        scales_again = held.tile([P, T], U8, name="scales_again", align_bytes=64)
         w_raw = held.tile([P, PACK, N], F32, name="w_raw", tag="weights_then_words", align_bytes=64)
         w_grouped = [held.tile([P, N // 2, PACK], BF16, name="w_grouped%d" % u, align_bytes=64) for u in range(2)]
         w_codes = held.tile([P, N], U32, name="w_codes", align_bytes=64)
@@ -41,16 +42,17 @@ def tile_picked_kvput_none_p_kernel(tc, x_words, x_scales, mem, w1, offs, slot, 
         nc.scalar.dma_start(all_words[:].bitcast(I32), x_words[0].rearrange("p c r -> p (c r)").bitcast(I32))
         nc.scalar.dma_start(w_raw[:], w1.rearrange("(p j) n -> p j n", j=PACK))
 
-        def gather_scales(h):
-            nc.vector.tensor_copy(picked_scales[h][:], all_scales[:].indirect(offs_sb[:, h * HALF // PER_COL : (h + 1) * HALF // PER_COL]))
+        def gather_scales(h, table):
+            nc.vector.tensor_copy(picked_scales[h][:], table[:].indirect(offs_sb[:, h * HALF // PER_COL : (h + 1) * HALF // PER_COL]))
 
         def move_scales(h):
             for q in range(4):
                 nc.sync.dma_start(plane[32 * q : 32 * q + 4, h * HALF : (h + 1) * HALF].bitcast(I32), picked_scales[h][112 + 4 * q : 116 + 4 * q, :].bitcast(I32))
 
-        gather_scales(0)
+        gather_scales(0, all_scales)
         move_scales(0)
-        gather_scales(1)
+        nc.vector.tensor_copy(scales_again[:].bitcast(I32), all_scales[:].bitcast(I32))
+        gather_scales(1, scales_again)
         cache = held.tile([P, U], F32, name="cache", tag="scales_then_cache", align_bytes=64)
         nc.sync.dma_start(cache[:], mem)
         move_scales(1)

@@ -10,13 +10,20 @@ U32 = mybir.dt.uint32
 U16 = mybir.dt.uint16
 U8 = mybir.dt.uint8
 FP8X4 = mybir.dt.float8_e4m3fn_x4
+COPY = mybir.ActivationFunctionType.Copy
+MIN = mybir.AluOpType.min
+MAX = mybir.AluOpType.max
 
 P = 128
 PACK = 4
-HALF = S // 2
 PER_COL = 16
-FIRST = 256
-WIDTHS = ((128, 128, 256), (256, 128, 128))
+SCALAR_PIECES = ((0, 320), (320, 384))
+VECTOR_PIECE = (704, 320)
+PASS_COLS = 256
+BANK = 512
+TOP = 3.4028234663852886e38
+MEM_COLS = 1024
+STORE_COLS = 512
 
 
 def tile_picked_kvput_none_p_kernel(tc, x_words, x_scales, mem, w1, offs, slot, out):
@@ -25,63 +32,81 @@ def tile_picked_kvput_none_p_kernel(tc, x_words, x_scales, mem, w1, offs, slot, 
         offs_sb = held.tile([P, S // PER_COL], U16, name="offs_sb")
         slot_sb = held.tile([P, S // PER_COL], U16, name="slot_sb")
         all_words = held.tile([P, T], U32, name="all_words", align_bytes=64)
-        all_scales = held.tile([P, T], U8, name="all_scales", tag="scales_then_cache", align_bytes=64)
-        scales_again = held.tile([P, T], U8, name="scales_again", align_bytes=64)
-        w_raw = held.tile([P, PACK, N], F32, name="w_raw", tag="weights_then_words", align_bytes=64)
-        w_grouped = [held.tile([P, N // 2, PACK], BF16, name="w_grouped%d" % u, align_bytes=64) for u in range(2)]
+        all_scales = held.tile([P, T], U8, name="all_scales", tag="scales_then_mem", align_bytes=64)
+        w_raw = held.tile([P, PACK, N], F32, name="w_raw", tag="weights_then_side", align_bytes=64)
+        w_grouped = held.tile([P, N, PACK], BF16, name="w_grouped", tag="weights_then_words", align_bytes=64)
         w_codes = held.tile([P, N], U32, name="w_codes", align_bytes=64)
         w_scales = held.tile([P, N], U8, name="w_scales", align_bytes=64)
-        picked_scales = [held.tile([P, HALF], U8, name="picked_scales%d" % h, align_bytes=64) for h in range(2)]
+        picked_scales = held.tile([P, S], U8, name="picked_scales", align_bytes=64)
         plane = held.tile([P, S], U8, name="plane", align_bytes=64)
+        cache = held.tile([P, U], F32, name="cache", align_bytes=64)
+        bottom = held.tile([P, max(n for j, n in SCALAR_PIECES)], F32, name="bottom", align_bytes=64)
 
+        def entries(lists, start, count):
+            return lists[:, start // PER_COL : (start + count) // PER_COL]
+
+        nc.gpsimd.memset(cache[:], TOP)
         nc.vector.memset(all_scales[0:112, :].bitcast(I32), 0)
         nc.vector.memset(plane[:].bitcast(I32), 0)
+        nc.scalar.dma_start(all_scales[112:P, :].bitcast(I32), x_scales[0].bitcast(I32))
         nc.sync.dma_start(offs_sb[:], offs)
         nc.sync.dma_start(slot_sb[:], slot)
-        nc.scalar.dma_start(all_scales[112:P, :].bitcast(I32), x_scales[0].bitcast(I32))
-        nc.scalar.dma_start(all_words[:].bitcast(I32), x_words[0].rearrange("p c r -> p (c r)").bitcast(I32))
-        nc.scalar.dma_start(w_raw[:], w1.rearrange("(p j) n -> p j n", j=PACK))
+        nc.sync.dma_start(w_raw[:], w1.rearrange("(p j) n -> p j n", j=PACK))
+        nc.sync.dma_start(all_words[:].bitcast(I32), x_words[0].rearrange("p c r -> p (c r)").bitcast(I32))
 
-        def gather_scales(h, table):
-            nc.vector.tensor_copy(picked_scales[h][:], table[:].indirect(offs_sb[:, h * HALF // PER_COL : (h + 1) * HALF // PER_COL]))
+        nc.scalar.activation(bottom[:], cache[:, 0 : bottom.shape[1]], COPY, scale=-1.0)
+        for j, n in SCALAR_PIECES:
+            nc.scalar.activation(cache[:].indirect(entries(slot_sb, j, n)), bottom[:, 0:n], COPY)
 
-        def move_scales(h):
-            for q in range(4):
-                nc.sync.dma_start(plane[32 * q : 32 * q + 4, h * HALF : (h + 1) * HALF].bitcast(I32), picked_scales[h][112 + 4 * q : 116 + 4 * q, :].bitcast(I32))
+        nc.vector.tensor_copy(picked_scales[:], all_scales[:].indirect(offs_sb[:]))
+        for q in range(4):
+            nc.sync.dma_start(plane[32 * q : 32 * q + 4, :].bitcast(I32), picked_scales[112 + 4 * q : 116 + 4 * q, :].bitcast(I32))
+        old = held.tile([P, U], F32, name="old", tag="scales_then_mem", align_bytes=64)
+        for c in range(0, U, MEM_COLS):
+            nc.sync.dma_start(old[:, c : c + MEM_COLS], mem[:, c : c + MEM_COLS])
 
-        gather_scales(0, all_scales)
-        move_scales(0)
-        nc.vector.tensor_copy(scales_again[:].bitcast(I32), all_scales[:].bitcast(I32))
-        gather_scales(1, scales_again)
-        cache = held.tile([P, U], F32, name="cache", tag="scales_then_cache", align_bytes=64)
-        nc.sync.dma_start(cache[:], mem)
-        move_scales(1)
-        for u in range(2):
-            cols = slice(u * N // 2, (u + 1) * N // 2)
-            nc.scalar.copy(w_grouped[u][:].rearrange("p (c i) j -> p c j i", i=4), w_raw[:, :, cols].rearrange("p j (c i) -> p c j i", i=4))
-            nc.vector.quantize_mx(out=w_codes[:, cols].bitcast(FP8X4), scales=w_scales[:, cols], in_=w_grouped[u][:].rearrange("p n j -> p (n j)"))
+        nc.vector.tensor_copy(w_grouped[:].rearrange("p (c i) j -> p c j i", i=4), w_raw[:].rearrange("p j (c i) -> p c j i", i=4))
+        side = held.tile([P, U], F32, name="side", tag="weights_then_side", align_bytes=64)
+        nc.vector.memset(side[:], -TOP)
+        nc.vector.quantize_mx(out=w_codes[:].bitcast(FP8X4), scales=w_scales[:], in_=w_grouped[:].rearrange("p n j -> p (n j)"))
 
-        y_first = held.tile([P, FIRST], F32, name="y_first", align_bytes=64)
-        y_rest = held.tile([P, S - FIRST], F32, name="y_rest", align_bytes=64)
-        j = 0
-        for h in range(2):
-            picked_words = held.tile([P, HALF], U32, name="picked_words%d" % h, tag="weights_then_words" if h else "first_words", align_bytes=64)
-            nc.vector.tensor_copy(picked_words[:], all_words[:].indirect(offs_sb[:, h * HALF // PER_COL : (h + 1) * HALF // PER_COL]))
-            c = 0
-            for width in WIDTHS[h]:
-                acc = psum.tile([P, width], F32, name="acc%d" % j)
+        first = SCALAR_PIECES[0][1]
+        first_words = held.tile([P, first], U32, name="first_words", tag="weights_then_words", align_bytes=64)
+        later_words = held.tile([P, S - first], U32, name="later_words", align_bytes=64)
+        nc.vector.tensor_copy(first_words[:], all_words[:].indirect(entries(offs_sb, 0, first)))
+        nc.vector.tensor_copy(later_words[:], all_words[:].indirect(entries(offs_sb, first, S - first)))
+        for c in range(0, U, MEM_COLS):
+            cols = slice(c, c + MEM_COLS)
+            nc.vector.tensor_tensor(cache[:, cols], old[:, cols], cache[:, cols], MIN)
+
+        def product(j, n, acc):
+            for c in range(0, n, PASS_COLS):
+                width = min(PASS_COLS, n - c)
+                words = later_words[:, j + c - first : j + c - first + width] if j else first_words[:, c : c + width]
                 nc.tensor.matmul_mx(
-                    out=acc[:],
+                    out=acc[:, c : c + width],
                     lhsT=w_codes[:].bitcast(FP8X4),
                     lhsT_scale=w_scales[:],
-                    rhs=picked_words[:, c : c + width].bitcast(FP8X4),
-                    rhs_scale=plane[:, j : j + width],
+                    rhs=words.bitcast(FP8X4),
+                    rhs_scale=plane[:, j + c : j + c + width],
                     start=True,
                     stop=True,
                 )
-                nc.scalar.copy(y_first[:, j : j + width] if j < FIRST else y_rest[:, j - FIRST : j - FIRST + width], acc[:])
-                c = c + width
-                j = j + width
-        nc.vector.tensor_copy(cache[:].indirect(slot_sb[:, 0 : FIRST // PER_COL]), y_first[:])
-        nc.vector.tensor_copy(cache[:].indirect(slot_sb[:, FIRST // PER_COL : S // PER_COL]), y_rest[:])
-        nc.sync.dma_start(out, cache[:])
+            y = held.tile([P, n], F32, name="y%d" % j, align_bytes=64)
+            nc.scalar.copy(y[:], acc[:, 0:n])
+            return y
+
+        acc_first = psum.tile([P, 2 * BANK], F32, name="acc_first", offset=0)
+        y_first = product(*SCALAR_PIECES[0], acc_first[:])
+        nc.scalar.activation(side[:].indirect(entries(slot_sb, *SCALAR_PIECES[0])), y_first[:], COPY)
+        acc_second = psum.tile([P, BANK], F32, name="acc_second", offset=0)
+        acc_last = psum.tile([P, BANK], F32, name="acc_last", offset=4 * BANK)
+        y_second = product(*SCALAR_PIECES[1], acc_second[:])
+        y_last = product(*VECTOR_PIECE, acc_last[:])
+        nc.scalar.activation(side[:].indirect(entries(slot_sb, *SCALAR_PIECES[1])), y_second[:], COPY)
+        nc.vector.tensor_copy(cache[:].indirect(entries(slot_sb, *VECTOR_PIECE)), y_last[:])
+        for c in range(0, U, STORE_COLS):
+            cols = slice(c, c + STORE_COLS)
+            merged = held.tile([P, STORE_COLS], F32, name="merged%d" % c, align_bytes=64)
+            nc.vector.tensor_tensor(merged[:], cache[:, cols], side[:, cols], MAX)
+            nc.sync.dma_start(out[:, cols], merged[:])

@@ -17,8 +17,8 @@ MAX = mybir.AluOpType.max
 P = 128
 PACK = 4
 PER_COL = 16
-SCALAR_PIECES = ((0, 320), (320, 384))
-VECTOR_PIECE = (704, 320)
+SCALAR_PIECES = ((0, 256), (256, 384))
+VECTOR_PIECE = (640, 384)
 PASS_COLS = 256
 BANK = 512
 TOP = 3.4028234663852886e38

@@ -12,6 +12,7 @@ U8 = mybir.dt.uint8
 FP8X4 = mybir.dt.float8_e4m3fn_x4
 COPY = mybir.ActivationFunctionType.Copy
 MIN = mybir.AluOpType.min
+ADD = mybir.AluOpType.add
 MAX = mybir.AluOpType.max
 
 P = 128
@@ -20,9 +21,9 @@ PER_COL = 16
 SCALAR_PIECES = ((0, 256), (256, 384))
 VECTOR_PIECE = (640, 384)
 PASS_COLS = 256
-BANK = 512
 TOP = 3.4028234663852886e38
-MEM_COLS = 1024
+MEM_PIECES = ((0, 768), (768, 1280))
+ON_GPSIMD = 768
 STORE_COLS = 512
 
 
@@ -45,7 +46,8 @@ def tile_picked_kvput_none_p_kernel(tc, x_words, x_scales, mem, w1, offs, slot, 
         def entries(lists, start, count):
             return lists[:, start // PER_COL : (start + count) // PER_COL]
 
-        nc.gpsimd.memset(cache[:], TOP)
+        nc.gpsimd.memset(cache[:, ON_GPSIMD:U], TOP)
+        nc.gpsimd.memset(cache[:, 0:ON_GPSIMD], 0.0)
         nc.vector.memset(all_scales[0:112, :].bitcast(I32), 0)
         nc.vector.memset(plane[:].bitcast(I32), 0)
         nc.scalar.dma_start(all_scales[112:P, :].bitcast(I32), x_scales[0].bitcast(I32))
@@ -54,7 +56,7 @@ def tile_picked_kvput_none_p_kernel(tc, x_words, x_scales, mem, w1, offs, slot, 
         nc.sync.dma_start(w_raw[:], w1.rearrange("(p j) n -> p j n", j=PACK))
         nc.sync.dma_start(all_words[:].bitcast(I32), x_words[0].rearrange("p c r -> p (c r)").bitcast(I32))
 
-        nc.scalar.activation(bottom[:], cache[:, 0 : bottom.shape[1]], COPY, scale=-1.0)
+        nc.scalar.activation(bottom[:], cache[:, U - bottom.shape[1] : U], COPY, scale=-1.0)
         for j, n in SCALAR_PIECES:
             nc.scalar.activation(cache[:].indirect(entries(slot_sb, j, n)), bottom[:, 0:n], COPY)
 
@@ -62,49 +64,48 @@ def tile_picked_kvput_none_p_kernel(tc, x_words, x_scales, mem, w1, offs, slot, 
         for q in range(4):
             nc.sync.dma_start(plane[32 * q : 32 * q + 4, :].bitcast(I32), picked_scales[112 + 4 * q : 116 + 4 * q, :].bitcast(I32))
         old = held.tile([P, U], F32, name="old", tag="scales_then_mem", align_bytes=64)
-        for c in range(0, U, MEM_COLS):
-            nc.sync.dma_start(old[:, c : c + MEM_COLS], mem[:, c : c + MEM_COLS])
+        for c, n in MEM_PIECES:
+            nc.sync.dma_start(old[:, c : c + n], mem[:, c : c + n])
 
         nc.vector.tensor_copy(w_grouped[:].rearrange("p (c i) j -> p c j i", i=4), w_raw[:].rearrange("p j (c i) -> p c j i", i=4))
         side = held.tile([P, U], F32, name="side", tag="weights_then_side", align_bytes=64)
         nc.vector.memset(side[:], -TOP)
         nc.vector.quantize_mx(out=w_codes[:].bitcast(FP8X4), scales=w_scales[:], in_=w_grouped[:].rearrange("p n j -> p (n j)"))
 
-        first = SCALAR_PIECES[0][1]
-        first_words = held.tile([P, first], U32, name="first_words", tag="weights_then_words", align_bytes=64)
-        later_words = held.tile([P, S - first], U32, name="later_words", align_bytes=64)
-        nc.vector.tensor_copy(first_words[:], all_words[:].indirect(entries(offs_sb, 0, first)))
-        nc.vector.tensor_copy(later_words[:], all_words[:].indirect(entries(offs_sb, first, S - first)))
-        for c in range(0, U, MEM_COLS):
-            cols = slice(c, c + MEM_COLS)
-            nc.vector.tensor_tensor(cache[:, cols], old[:, cols], cache[:, cols], MIN)
+        picked = {}
+        for j, n in (SCALAR_PIECES[0], VECTOR_PIECE, SCALAR_PIECES[1]):
+            picked[j] = held.tile([P, n], U32, name="picked%d" % j, tag="picked%d" % j if j else "weights_then_words", align_bytes=64)
+            nc.vector.tensor_copy(picked[j][:], all_words[:].indirect(entries(offs_sb, j, n)))
+        for c, n in MEM_PIECES:
+            cols = slice(c, c + n)
+            if c < ON_GPSIMD:
+                nc.gpsimd.tensor_tensor(cache[:, cols], old[:, cols], cache[:, cols], ADD)
+            else:
+                nc.vector.tensor_tensor(cache[:, cols], old[:, cols], cache[:, cols], MIN)
 
-        def product(j, n, acc):
+        def product(j, n, bank):
+            acc = psum.tile([P, n], F32, name="acc%d" % j, tag=bank)
             for c in range(0, n, PASS_COLS):
                 width = min(PASS_COLS, n - c)
-                words = later_words[:, j + c - first : j + c - first + width] if j else first_words[:, c : c + width]
                 nc.tensor.matmul_mx(
                     out=acc[:, c : c + width],
                     lhsT=w_codes[:].bitcast(FP8X4),
                     lhsT_scale=w_scales[:],
-                    rhs=words.bitcast(FP8X4),
+                    rhs=picked[j][:, c : c + width].bitcast(FP8X4),
                     rhs_scale=plane[:, j + c : j + c + width],
                     start=True,
                     stop=True,
                 )
-            y = held.tile([P, n], F32, name="y%d" % j, align_bytes=64)
-            nc.scalar.copy(y[:], acc[:, 0:n])
-            return y
+            return acc
 
-        acc_first = psum.tile([P, 2 * BANK], F32, name="acc_first", offset=0)
-        y_first = product(*SCALAR_PIECES[0], acc_first[:])
-        nc.scalar.activation(side[:].indirect(entries(slot_sb, *SCALAR_PIECES[0])), y_first[:], COPY)
-        acc_second = psum.tile([P, BANK], F32, name="acc_second", offset=0)
-        acc_last = psum.tile([P, BANK], F32, name="acc_last", offset=4 * BANK)
-        y_second = product(*SCALAR_PIECES[1], acc_second[:])
-        y_last = product(*VECTOR_PIECE, acc_last[:])
-        nc.scalar.activation(side[:].indirect(entries(slot_sb, *SCALAR_PIECES[1])), y_second[:], COPY)
-        nc.vector.tensor_copy(cache[:].indirect(entries(slot_sb, *VECTOR_PIECE)), y_last[:])
+        for j, n in SCALAR_PIECES:
+            y = held.tile([P, n], F32, name="y%d" % j, align_bytes=64)
+            nc.scalar.copy(y[:], product(j, n, "scalar_bank")[:])
+            nc.scalar.activation(side[:].indirect(entries(slot_sb, j, n)), y[:], COPY)
+        j, n = VECTOR_PIECE
+        y = held.tile([P, n], F32, name="y%d" % j, align_bytes=64)
+        nc.vector.tensor_copy(y[:], product(j, n, "vector_bank")[:])
+        nc.vector.tensor_copy(cache[:].indirect(entries(slot_sb, j, n)), y[:])
         for c in range(0, U, STORE_COLS):
             cols = slice(c, c + STORE_COLS)
             merged = held.tile([P, STORE_COLS], F32, name="merged%d" % c, align_bytes=64)

@@ -22,8 +22,8 @@ SCALAR_PIECES = ((0, 256), (256, 384))
 VECTOR_PIECE = (640, 384)
 PASS_COLS = 256
 TOP = 3.4028234663852886e38
-MEM_PIECES = ((0, 768), (768, 1280))
-ON_GPSIMD = 768
+LEAD = 256
+ON_GPSIMD = 896
 STORE_COLS = 512
 
 
@@ -56,6 +56,9 @@ def tile_picked_kvput_none_p_kernel(tc, x_words, x_scales, mem, w1, offs, slot, 
         nc.sync.dma_start(w_raw[:], w1.rearrange("(p j) n -> p j n", j=PACK))
         nc.sync.dma_start(all_words[:].bitcast(I32), x_words[0].rearrange("p c r -> p (c r)").bitcast(I32))
 
+        lead = held.tile([P, LEAD], F32, name="lead", align_bytes=64)
+        nc.sync.dma_start(lead[:], mem[:, 0:LEAD])
+
         nc.scalar.activation(bottom[:], cache[:, U - bottom.shape[1] : U], COPY, scale=-1.0)
         for j, n in SCALAR_PIECES:
             nc.scalar.activation(cache[:].indirect(entries(slot_sb, j, n)), bottom[:, 0:n], COPY)
@@ -63,9 +66,9 @@ def tile_picked_kvput_none_p_kernel(tc, x_words, x_scales, mem, w1, offs, slot, 
         nc.vector.tensor_copy(picked_scales[:], all_scales[:].indirect(offs_sb[:]))
         for q in range(4):
             nc.sync.dma_start(plane[32 * q : 32 * q + 4, :].bitcast(I32), picked_scales[112 + 4 * q : 116 + 4 * q, :].bitcast(I32))
-        old = held.tile([P, U], F32, name="old", tag="scales_then_mem", align_bytes=64)
-        for c, n in MEM_PIECES:
-            nc.sync.dma_start(old[:, c : c + n], mem[:, c : c + n])
+        old = held.tile([P, U - LEAD], F32, name="old", tag="scales_then_mem", align_bytes=64)
+        nc.sync.dma_start(old[:, 0 : ON_GPSIMD - LEAD], mem[:, LEAD:ON_GPSIMD])
+        nc.sync.dma_start(old[:, ON_GPSIMD - LEAD : U - LEAD], mem[:, ON_GPSIMD:U])
 
         nc.vector.tensor_copy(w_grouped[:].rearrange("p (c i) j -> p c j i", i=4), w_raw[:].rearrange("p j (c i) -> p c j i", i=4))
         side = held.tile([P, U], F32, name="side", tag="weights_then_side", align_bytes=64)
@@ -76,12 +79,9 @@ def tile_picked_kvput_none_p_kernel(tc, x_words, x_scales, mem, w1, offs, slot, 
         for j, n in (SCALAR_PIECES[0], VECTOR_PIECE, SCALAR_PIECES[1]):
             picked[j] = held.tile([P, n], U32, name="picked%d" % j, tag="picked%d" % j if j else "weights_then_words", align_bytes=64)
             nc.vector.tensor_copy(picked[j][:], all_words[:].indirect(entries(offs_sb, j, n)))
-        for c, n in MEM_PIECES:
-            cols = slice(c, c + n)
-            if c < ON_GPSIMD:
-                nc.gpsimd.tensor_tensor(cache[:, cols], old[:, cols], cache[:, cols], ADD)
-            else:
-                nc.vector.tensor_tensor(cache[:, cols], old[:, cols], cache[:, cols], MIN)
+        nc.gpsimd.tensor_tensor(cache[:, 0:LEAD], lead[:], cache[:, 0:LEAD], ADD)
+        nc.gpsimd.tensor_tensor(cache[:, LEAD:ON_GPSIMD], old[:, 0 : ON_GPSIMD - LEAD], cache[:, LEAD:ON_GPSIMD], ADD)
+        nc.vector.tensor_tensor(cache[:, ON_GPSIMD:U], old[:, ON_GPSIMD - LEAD : U - LEAD], cache[:, ON_GPSIMD:U], MIN)
 
         def product(j, n, bank):
             acc = psum.tile([P, n], F32, name="acc%d" % j, tag=bank)

@@ -50,7 +50,7 @@ def tile_picked_kvput_none_p_kernel(tc, x_words, x_scales, mem, w1, offs, slot, 
         nc.gpsimd.memset(cache[:, 0:ON_GPSIMD], 0.0)
         nc.vector.memset(all_scales[0:112, :].bitcast(I32), 0)
         nc.vector.memset(plane[:].bitcast(I32), 0)
-        nc.scalar.dma_start(all_scales[112:P, :].bitcast(I32), x_scales[0].bitcast(I32))
+        nc.sync.dma_start(all_scales[112:P, :].bitcast(I32), x_scales[0].bitcast(I32))
         nc.sync.dma_start(offs_sb[:], offs)
         nc.sync.dma_start(slot_sb[:], slot)
         nc.sync.dma_start(w_raw[:], w1.rearrange("(p j) n -> p j n", j=PACK))
@@ -83,28 +83,33 @@ def tile_picked_kvput_none_p_kernel(tc, x_words, x_scales, mem, w1, offs, slot, 
         nc.gpsimd.tensor_tensor(cache[:, LEAD:ON_GPSIMD], old[:, 0 : ON_GPSIMD - LEAD], cache[:, LEAD:ON_GPSIMD], ADD)
         nc.vector.tensor_tensor(cache[:, ON_GPSIMD:U], old[:, ON_GPSIMD - LEAD : U - LEAD], cache[:, ON_GPSIMD:U], MIN)
 
-        def product(j, n, bank):
-            acc = psum.tile([P, n], F32, name="acc%d" % j, tag=bank)
-            for c in range(0, n, PASS_COLS):
-                width = min(PASS_COLS, n - c)
+        def product(j, c, n, bank):
+            acc = psum.tile([P, n], F32, name="acc%d" % (j + c), tag=bank)
+            for d in range(0, n, PASS_COLS):
+                width = min(PASS_COLS, n - d)
                 nc.tensor.matmul_mx(
-                    out=acc[:, c : c + width],
+                    out=acc[:, d : d + width],
                     lhsT=w_codes[:].bitcast(FP8X4),
                     lhsT_scale=w_scales[:],
-                    rhs=picked[j][:, c : c + width].bitcast(FP8X4),
-                    rhs_scale=plane[:, j + c : j + c + width],
+                    rhs=picked[j][:, c + d : c + d + width].bitcast(FP8X4),
+                    rhs_scale=plane[:, j + c + d : j + c + d + width],
                     start=True,
                     stop=True,
                 )
             return acc
 
-        for j, n in SCALAR_PIECES:
-            y = held.tile([P, n], F32, name="y%d" % j, align_bytes=64)
-            nc.scalar.copy(y[:], product(j, n, "scalar_bank")[:])
-            nc.scalar.activation(side[:].indirect(entries(slot_sb, j, n)), y[:], COPY)
+        j, n = SCALAR_PIECES[0]
+        y = held.tile([P, n], F32, name="y%d" % j, align_bytes=64)
+        nc.scalar.copy(y[:, 0 : n // 2], product(j, 0, n // 2, "lead_bank")[:])
+        nc.scalar.copy(y[:, n // 2 : n], product(j, n // 2, n // 2, "scalar_bank")[:])
+        nc.scalar.activation(side[:].indirect(entries(slot_sb, j, n)), y[:], COPY)
+        j, n = SCALAR_PIECES[1]
+        y = held.tile([P, n], F32, name="y%d" % j, align_bytes=64)
+        nc.scalar.copy(y[:], product(j, 0, n, "scalar_bank")[:])
+        nc.scalar.activation(side[:].indirect(entries(slot_sb, j, n)), y[:], COPY)
         j, n = VECTOR_PIECE
         y = held.tile([P, n], F32, name="y%d" % j, align_bytes=64)
-        nc.vector.tensor_copy(y[:], product(j, n, "vector_bank")[:])
+        nc.vector.tensor_copy(y[:], product(j, 0, n, "vector_bank")[:])
         nc.vector.tensor_copy(cache[:].indirect(entries(slot_sb, j, n)), y[:])
         for c in range(0, U, STORE_COLS):
             cols = slice(c, c + STORE_COLS)

@@ -22,8 +22,8 @@ SCALAR_PIECES = ((0, 256), (256, 384))
 VECTOR_PIECE = (640, 384)
 PASS_COLS = 256
 TOP = 3.4028234663852886e38
-LEAD = 256
-ON_GPSIMD = 896
+LEAD = 384
+ON_GPSIMD = 960
 STORE_COLS = 512
 
 

@@ -46,10 +46,10 @@ def tile_picked_kvput_none_p_kernel(tc, x_words, x_scales, mem, w1, offs, slot, 
         def entries(lists, start, count):
             return lists[:, start // PER_COL : (start + count) // PER_COL]
 
-        nc.gpsimd.memset(cache[:, ON_GPSIMD:U], TOP)
-        nc.gpsimd.memset(cache[:, 0:ON_GPSIMD], 0.0)
         nc.vector.memset(all_scales[0:112, :].bitcast(I32), 0)
         nc.vector.memset(plane[:].bitcast(I32), 0)
+        nc.vector.memset(cache[:, ON_GPSIMD:U], TOP)
+        nc.vector.memset(cache[:, 0:ON_GPSIMD], 0.0)
         nc.sync.dma_start(all_scales[112:P, :].bitcast(I32), x_scales[0].bitcast(I32))
         nc.sync.dma_start(offs_sb[:], offs)
         nc.sync.dma_start(slot_sb[:], slot)

@@ -34,7 +34,7 @@ def tile_picked_kvput_none_p_kernel(tc, x_words, x_scales, mem, w1, offs, slot, 
         slot_sb = held.tile([P, S // PER_COL], U16, name="slot_sb")
         all_words = held.tile([P, T], U32, name="all_words", align_bytes=64)
         all_scales = held.tile([P, T], U8, name="all_scales", tag="scales_then_mem", align_bytes=64)
-        w_raw = held.tile([P, PACK, N], F32, name="w_raw", tag="weights_then_side", align_bytes=64)
+        w_raw = held.tile([P, PACK, N], F32, name="w_raw", align_bytes=64)
         w_grouped = held.tile([P, N, PACK], BF16, name="w_grouped", tag="weights_then_words", align_bytes=64)
         w_codes = held.tile([P, N], U32, name="w_codes", align_bytes=64)
         w_scales = held.tile([P, N], U8, name="w_scales", align_bytes=64)
@@ -50,6 +50,8 @@ def tile_picked_kvput_none_p_kernel(tc, x_words, x_scales, mem, w1, offs, slot, 
         nc.vector.memset(plane[:].bitcast(I32), 0)
         nc.vector.memset(cache[:, ON_GPSIMD:U], TOP)
         nc.vector.memset(cache[:, 0:ON_GPSIMD], 0.0)
+        side = held.tile([P, U], F32, name="side", align_bytes=64)
+        nc.vector.memset(side[:], -TOP)
         nc.sync.dma_start(all_scales[112:P, :].bitcast(I32), x_scales[0].bitcast(I32))
         nc.sync.dma_start(offs_sb[:], offs)
         nc.sync.dma_start(slot_sb[:], slot)
@@ -71,8 +73,6 @@ def tile_picked_kvput_none_p_kernel(tc, x_words, x_scales, mem, w1, offs, slot, 
         nc.sync.dma_start(old[:, ON_GPSIMD - LEAD : U - LEAD], mem[:, ON_GPSIMD:U])
 
         nc.vector.tensor_copy(w_grouped[:].rearrange("p (c i) j -> p c j i", i=4), w_raw[:].rearrange("p j (c i) -> p c j i", i=4))
-        side = held.tile([P, U], F32, name="side", tag="weights_then_side", align_bytes=64)
-        nc.vector.memset(side[:], -TOP)
         nc.vector.quantize_mx(out=w_codes[:].bitcast(FP8X4), scales=w_scales[:], in_=w_grouped[:].rearrange("p n j -> p (n j)"))
 
         picked = {}

@@ -55,7 +55,7 @@ def tile_picked_kvput_none_p_kernel(tc, x_words, x_scales, mem, w1, offs, slot, 
         nc.sync.dma_start(all_scales[112:P, :].bitcast(I32), x_scales[0].bitcast(I32))
         nc.sync.dma_start(offs_sb[:], offs)
         nc.sync.dma_start(slot_sb[:], slot)
-        nc.sync.dma_start(w_raw[:], w1.rearrange("(p j) n -> p j n", j=PACK))
+        nc.scalar.dma_start(w_raw[:], w1.rearrange("(p j) n -> p j n", j=PACK))
         nc.sync.dma_start(all_words[:].bitcast(I32), x_words[0].rearrange("p c r -> p (c r)").bitcast(I32))
 
         lead = held.tile([P, LEAD], F32, name="lead", align_bytes=64)

@@ -46,16 +46,15 @@ def tile_picked_kvput_none_p_kernel(tc, x_words, x_scales, mem, w1, offs, slot, 
         def entries(lists, start, count):
             return lists[:, start // PER_COL : (start + count) // PER_COL]
 
-        nc.vector.memset(all_scales[0:112, :].bitcast(I32), 0)
-        nc.vector.memset(plane[:].bitcast(I32), 0)
+        nc.vector.memset(all_scales[:].bitcast(I32), 0)
         nc.vector.memset(cache[:, ON_GPSIMD:U], TOP)
         nc.vector.memset(cache[:, 0:ON_GPSIMD], 0.0)
         side = held.tile([P, U], F32, name="side", align_bytes=64)
         nc.vector.memset(side[:], -TOP)
-        nc.sync.dma_start(all_scales[112:P, :].bitcast(I32), x_scales[0].bitcast(I32))
-        nc.sync.dma_start(offs_sb[:], offs)
+        nc.sync.dma_start(w_raw[:], w1.rearrange("(p j) n -> p j n", j=PACK))
         nc.sync.dma_start(slot_sb[:], slot)
-        nc.scalar.dma_start(w_raw[:], w1.rearrange("(p j) n -> p j n", j=PACK))
+        nc.sync.dma_start(offs_sb[:], offs)
+        nc.sync.dma_start(all_scales[0:P:8, :].bitcast(I32), x_scales[0].bitcast(I32))
         nc.sync.dma_start(all_words[:].bitcast(I32), x_words[0].rearrange("p c r -> p (c r)").bitcast(I32))
 
         lead = held.tile([P, LEAD], F32, name="lead", align_bytes=64)
@@ -66,8 +65,9 @@ def tile_picked_kvput_none_p_kernel(tc, x_words, x_scales, mem, w1, offs, slot, 
             nc.scalar.activation(cache[:].indirect(entries(slot_sb, j, n)), bottom[:, 0:n], COPY)
 
         nc.vector.tensor_copy(picked_scales[:], all_scales[:].indirect(offs_sb[:]))
-        for q in range(4):
-            nc.sync.dma_start(plane[32 * q : 32 * q + 4, :].bitcast(I32), picked_scales[112 + 4 * q : 116 + 4 * q, :].bitcast(I32))
+        nc.vector.tensor_copy(plane[:].bitcast(I32), picked_scales[:].bitcast(I32))
+        for r in range(1, 4):
+            nc.sync.dma_start(plane[r:P:32, :].bitcast(I32), picked_scales[8 * r : P : 32, :].bitcast(I32))
         old = held.tile([P, U - LEAD], F32, name="old", tag="scales_then_mem", align_bytes=64)
         nc.sync.dma_start(old[:, 0 : ON_GPSIMD - LEAD], mem[:, LEAD:ON_GPSIMD])
         nc.sync.dma_start(old[:, ON_GPSIMD - LEAD : U - LEAD], mem[:, ON_GPSIMD:U])

@@ -24,7 +24,7 @@ PASS_COLS = 256
 TOP = 3.4028234663852886e38
 LEAD = 384
 ON_GPSIMD = 960
-STORE_COLS = 512
+STORES = (256, 256, 512, 512, 512)
 
 
 def tile_picked_kvput_none_p_kernel(tc, x_words, x_scales, mem, w1, offs, slot, out):
@@ -111,8 +111,9 @@ def tile_picked_kvput_none_p_kernel(tc, x_words, x_scales, mem, w1, offs, slot, 
         y = held.tile([P, n], F32, name="y%d" % j, align_bytes=64)
         nc.vector.tensor_copy(y[:], product(j, 0, n, "vector_bank")[:])
         nc.vector.tensor_copy(cache[:].indirect(entries(slot_sb, j, n)), y[:])
-        for c in range(0, U, STORE_COLS):
-            cols = slice(c, c + STORE_COLS)
-            merged = held.tile([P, STORE_COLS], F32, name="merged%d" % c, align_bytes=64)
+        for k, width in enumerate(STORES):
+            c = sum(STORES[:k])
+            cols = slice(c, c + width)
+            merged = held.tile([P, width], F32, name="merged%d" % c, align_bytes=64)
             nc.vector.tensor_tensor(merged[:], cache[:, cols], side[:, cols], MAX)
             nc.sync.dma_start(out[:, cols], merged[:])

import concourse.mybir as mybir

K, T, S, N, U = 512, 4096, 1024, 128, 2048
FLOPS = 2 * K * N * S

F32 = mybir.dt.float32
BF16 = mybir.dt.bfloat16
I32 = mybir.dt.int32
U32 = mybir.dt.uint32
U16 = mybir.dt.uint16
U8 = mybir.dt.uint8
FP8X4 = mybir.dt.float8_e4m3fn_x4
COPY = mybir.ActivationFunctionType.Copy
MIN = mybir.AluOpType.min
ADD = mybir.AluOpType.add
MAX = mybir.AluOpType.max

P = 128
PACK = 4
PER_COL = 16
SCALAR_PIECES = ((0, 256), (256, 384))
VECTOR_PIECE = (640, 384)
PASS_COLS = 256
TOP = 3.4028234663852886e38
LEAD = 384
ON_GPSIMD = 960
STORES = (256, 256, 512, 512, 512)


def tile_picked_kvput_none_p_kernel(tc, x_words, x_scales, mem, w1, offs, slot, out):
    nc = tc.nc
    with tc.tile_pool(name="held", bufs=1) as held, tc.psum_pool(name="psum", bufs=1) as psum:
        offs_sb = held.tile([P, S // PER_COL], U16, name="offs_sb")
        slot_sb = held.tile([P, S // PER_COL], U16, name="slot_sb")
        all_words = held.tile([P, T], U32, name="all_words", align_bytes=64)
        all_scales = held.tile([P, T], U8, name="all_scales", tag="scales_then_mem", align_bytes=64)
        w_raw = held.tile([P, PACK, N], F32, name="w_raw", align_bytes=64)
        w_grouped = held.tile([P, N, PACK], BF16, name="w_grouped", tag="weights_then_words", align_bytes=64)
        w_codes = held.tile([P, N], U32, name="w_codes", align_bytes=64)
        w_scales = held.tile([P, N], U8, name="w_scales", align_bytes=64)
        picked_scales = held.tile([P, S], U8, name="picked_scales", align_bytes=64)
        plane = held.tile([P, S], U8, name="plane", align_bytes=64)
        cache = held.tile([P, U], F32, name="cache", align_bytes=64)
        bottom = held.tile([P, max(n for j, n in SCALAR_PIECES)], F32, name="bottom", align_bytes=64)

        def entries(lists, start, count):
            return lists[:, start // PER_COL : (start + count) // PER_COL]

        nc.vector.memset(all_scales[:].bitcast(I32), 0)
        nc.vector.memset(cache[:, ON_GPSIMD:U], TOP)
        nc.vector.memset(cache[:, 0:ON_GPSIMD], 0.0)
        side = held.tile([P, U], F32, name="side", align_bytes=64)
        nc.vector.memset(side[:], -TOP)
        nc.sync.dma_start(w_raw[:], w1.rearrange("(p j) n -> p j n", j=PACK))
        nc.sync.dma_start(slot_sb[:], slot)
        nc.sync.dma_start(offs_sb[:], offs)
        nc.sync.dma_start(all_scales[0:P:8, :].bitcast(I32), x_scales[0].bitcast(I32))
        nc.sync.dma_start(all_words[:].bitcast(I32), x_words[0].rearrange("p c r -> p (c r)").bitcast(I32))

        lead = held.tile([P, LEAD], F32, name="lead", align_bytes=64)
        nc.sync.dma_start(lead[:], mem[:, 0:LEAD])

        nc.scalar.activation(bottom[:], cache[:, U - bottom.shape[1] : U], COPY, scale=-1.0)
        for j, n in SCALAR_PIECES:
            nc.scalar.activation(cache[:].indirect(entries(slot_sb, j, n)), bottom[:, 0:n], COPY)

        nc.vector.tensor_copy(picked_scales[:], all_scales[:].indirect(offs_sb[:]))
        nc.vector.tensor_copy(plane[:].bitcast(I32), picked_scales[:].bitcast(I32))
        for r in range(1, 4):
            nc.sync.dma_start(plane[r:P:32, :].bitcast(I32), picked_scales[8 * r : P : 32, :].bitcast(I32))
        old = held.tile([P, U - LEAD], F32, name="old", tag="scales_then_mem", align_bytes=64)
        nc.sync.dma_start(old[:, 0 : ON_GPSIMD - LEAD], mem[:, LEAD:ON_GPSIMD])
        nc.sync.dma_start(old[:, ON_GPSIMD - LEAD : U - LEAD], mem[:, ON_GPSIMD:U])

        nc.vector.tensor_copy(w_grouped[:].rearrange("p (c i) j -> p c j i", i=4), w_raw[:].rearrange("p j (c i) -> p c j i", i=4))
        nc.vector.quantize_mx(out=w_codes[:].bitcast(FP8X4), scales=w_scales[:], in_=w_grouped[:].rearrange("p n j -> p (n j)"))

        picked = {}
        for j, n in (SCALAR_PIECES[0], VECTOR_PIECE, SCALAR_PIECES[1]):
            picked[j] = held.tile([P, n], U32, name="picked%d" % j, tag="picked%d" % j if j else "weights_then_words", align_bytes=64)
            nc.vector.tensor_copy(picked[j][:], all_words[:].indirect(entries(offs_sb, j, n)))
        nc.gpsimd.tensor_tensor(cache[:, 0:LEAD], lead[:], cache[:, 0:LEAD], ADD)
        nc.gpsimd.tensor_tensor(cache[:, LEAD:ON_GPSIMD], old[:, 0 : ON_GPSIMD - LEAD], cache[:, LEAD:ON_GPSIMD], ADD)
        nc.vector.tensor_tensor(cache[:, ON_GPSIMD:U], old[:, ON_GPSIMD - LEAD : U - LEAD], cache[:, ON_GPSIMD:U], MIN)

        def product(j, c, n, bank):
            acc = psum.tile([P, n], F32, name="acc%d" % (j + c), tag=bank)
            for d in range(0, n, PASS_COLS):
                width = min(PASS_COLS, n - d)
                nc.tensor.matmul_mx(
                    out=acc[:, d : d + width],
                    lhsT=w_codes[:].bitcast(FP8X4),
                    lhsT_scale=w_scales[:],
                    rhs=picked[j][:, c + d : c + d + width].bitcast(FP8X4),
                    rhs_scale=plane[:, j + c + d : j + c + d + width],
                    start=True,
                    stop=True,
                )
            return acc

        j, n = SCALAR_PIECES[0]
        y = held.tile([P, n], F32, name="y%d" % j, align_bytes=64)
        nc.scalar.copy(y[:, 0 : n // 2], product(j, 0, n // 2, "lead_bank")[:])
        nc.scalar.copy(y[:, n // 2 : n], product(j, n // 2, n // 2, "scalar_bank")[:])
        nc.scalar.activation(side[:].indirect(entries(slot_sb, j, n)), y[:], COPY)
        j, n = SCALAR_PIECES[1]
        y = held.tile([P, n], F32, name="y%d" % j, align_bytes=64)
        nc.scalar.copy(y[:], product(j, 0, n, "scalar_bank")[:])
        nc.scalar.activation(side[:].indirect(entries(slot_sb, j, n)), y[:], COPY)
        j, n = VECTOR_PIECE
        y = held.tile([P, n], F32, name="y%d" % j, align_bytes=64)
        nc.vector.tensor_copy(y[:], product(j, 0, n, "vector_bank")[:])
        nc.vector.tensor_copy(cache[:].indirect(entries(slot_sb, j, n)), y[:])
        for k, width in enumerate(STORES):
            c = sum(STORES[:k])
            cols = slice(c, c + width)
            merged = held.tile([P, width], F32, name="merged%d" % c, align_bytes=64)
            nc.vector.tensor_tensor(merged[:], cache[:, cols], side[:, cols], MAX)
            nc.sync.dma_start(out[:, cols], merged[:])
